import numpy as np, ml_dtypes
CORES = [3,19,35,51,67,83,99,115]
N = 8
def setup_inputs(rng):
    return {"x": rng.standard_normal((N, 128, 8192), dtype=np.float32).astype(ml_dtypes.bfloat16)}
def reference(x):
    s = x.sum(axis=0, dtype=np.float64).astype(x.dtype)
    return {"y": np.broadcast_to(s, (N,) + s.shape)}

@@ -1,0 +1,104 @@
+import concourse.bass as bass
+STAGES = [16] * 8
+S = 16
+RAILS = True
+NR = 1
+PRE = 2
+K = len(STAGES)
+OFF = [sum(STAGES[:k]) for k in range(K)]
+SIZES = sorted(set(STAGES))
+CLS = [SIZES.index(r) for r in STAGES]
+IDX = [CLS[:k].count(CLS[k]) for k in range(K)]
+
+def shape_of(c):
+    if c >= len(SIZES):
+        return [1, 128, 1]
+    return [CLS.count(c) * S, 128, SIZES[c] * 8192 // (S * 128)]
+SCRATCH = {'xa': ('dram', shape_of(0), 'bfloat16'), 'ra': ('dram', shape_of(0), 'bfloat16'), 'xb': ('dram', shape_of(1), 'bfloat16'), 'rb': ('dram', shape_of(1), 'bfloat16'), 'xc': ('dram', shape_of(2), 'bfloat16'), 'rc': ('dram', shape_of(2), 'bfloat16')}
+SEMAPHORES = ['st', 'sent'] + ['s%d' % k for k in range(16)] + ['ld%d' % k for k in range(16)]
+
+def red_core(k, s):
+    if RAILS:
+        j, h = divmod(s, 2)
+        return (2 * j + 1) * 8 + (6 if h else 2) + k % 2
+    return 2 * s * 8 + 4 + (3 - k % NR)
+
+def fwd_core(rank_core, s):
+    if RAILS and s % 2:
+        return rank_core // 8 * 8 + 6 + s // 2 % 2
+    return None
+
+def bits(first, n):
+    return (1 << n) - 1 << first
+
+def rank_program(g, core, T, topo):
+    sems = [T.sem.s0, T.sem.s1, T.sem.s2, T.sem.s3, T.sem.s4, T.sem.s5, T.sem.s6, T.sem.s7, T.sem.s8, T.sem.s9, T.sem.s10, T.sem.s11, T.sem.s12, T.sem.s13, T.sem.s14, T.sem.s15]
+    lds = [T.sem.ld0, T.sem.ld1, T.sem.ld2, T.sem.ld3, T.sem.ld4, T.sem.ld5, T.sem.ld6, T.sem.ld7, T.sem.ld8, T.sem.ld9, T.sem.ld10, T.sem.ld11, T.sem.ld12, T.sem.ld13, T.sem.ld14, T.sem.ld15]
+    xbuf = [T.xa, T.xb, T.xc]
+    rbuf = [T.ra, T.rb, T.rc]
+    ranks = list(T.cores)
+
+    def piece(k, s):
+        return xbuf[CLS[k]][IDX[k] * S + s]
+
+    def landed(k, i):
+        return xbuf[CLS[k]][IDX[k] * 8 + i]
+
+    def did(c):
+        rid, pid, se = topo.addr(c)
+        return bass.DstId(rid=rid, pnc=pid)
+
+    def copy(src, dst, dst_core, mask, sem):
+        return bass.RemoteDMATransfer(dst_ids=[did(dst_core)], dma_engine_mask=mask, remote_sem=sem, src=src, dst=dst)
+    direct = [s for s in range(S) if fwd_core(ranks[0], s) is None]
+    passed = [s for s in range(S) if fwd_core(ranks[0], s) is not None]
+    e_dir = 8 // len(direct)
+    e_pas = 8 // len(passed) if passed else 0
+    sent = 0
+    rank = T.rank_of(core)
+    if rank is not None:
+
+        def load(k):
+            g.dma_start(xbuf[CLS[k]][IDX[k] * S:(IDX[k] + 1) * S], T.x[OFF[k]:OFF[k] + STAGES[k], :]).then_inc(lds[k], 16)
+        for k in range(min(PRE, K)):
+            load(k)
+        for k in range(K):
+            g.wait_ge(lds[k], 16)
+            tr = []
+            for n, s in enumerate(direct):
+                tr.append(copy(piece(k, s), landed(k, rank), red_core(k, s), bits(n * e_dir, e_dir), sems[k]))
+                sent += e_dir
+            for n, s in enumerate(passed):
+                tr.append(copy(piece(k, s), piece(k, s), fwd_core(core, s), bits(8 + n * e_pas, e_pas), sems[k]))
+                sent += e_pas
+            g.remote_dma_fused(tr, local_sem=T.sem.sent)
+            if k + PRE < K:
+                load(k + PRE)
+        for k in range(K):
+            g.wait_ge(sems[k], 8 * S)
+            g.dma_start(T.y[OFF[k]:OFF[k] + STAGES[k], :], rbuf[CLS[k]][IDX[k] * S:(IDX[k] + 1) * S]).then_inc(T.sem.st, 16)
+        g.wait_ge(T.sem.st, 16 * K)
+        g.wait_ge(T.sem.sent, sent)
+        return
+    home = [r for r in ranks if r // 8 == core // 8]
+    mine = [s for s in passed if home and fwd_core(home[0], s) == core]
+    if mine:
+        e_fwd = 8 // len(mine)
+        i = T.rank_of(home[0])
+        for k in range(K):
+            g.wait_ge(sems[k], e_pas * len(mine))
+            tr = [copy(piece(k, s), landed(k, i), red_core(k, s), bits(n * e_fwd, e_fwd), sems[k]) for n, s in enumerate(mine)]
+            sent += e_fwd * len(mine)
+            g.remote_dma_fused(tr, local_sem=T.sem.sent)
+        g.wait_ge(T.sem.sent, sent)
+        return
+    n_fwd = len([s for s in passed if fwd_core(ranks[0], s) == fwd_core(ranks[0], passed[0])]) if passed else 1
+    for k in range(K):
+        for s in range(S):
+            if red_core(k, s) != core:
+                continue
+            g.wait_ge(sems[k], 8 * (e_dir if s in direct else 8 // n_fwd))
+            g.remote_dma_fused([bass.RemoteDMATransfer(dst_ids=[did(r) for r in ranks], dma_engine_mask=255, remote_sem=sems[k], srcs=[landed(k, i) for i in range(8)], dsts=[rbuf[CLS[k]][IDX[k] * S + s] for r in ranks], alu_op=1)], local_sem=T.sem.sent)
+            sent += 8
+    if sent:
+        g.wait_ge(T.sem.sent, sent)

@@ -1,35 +1,39 @@
 import concourse.bass as bass
 STAGES = [16] * 8
 S = 16
-RAILS = True
-NR = 1
-PRE = 2
 K = len(STAGES)
 OFF = [sum(STAGES[:k]) for k in range(K)]
 SIZES = sorted(set(STAGES))
 CLS = [SIZES.index(r) for r in STAGES]
 IDX = [CLS[:k].count(CLS[k]) for k in range(K)]
 
+
 def shape_of(c):
     if c >= len(SIZES):
         return [1, 128, 1]
     return [CLS.count(c) * S, 128, SIZES[c] * 8192 // (S * 128)]
-SCRATCH = {'xa': ('dram', shape_of(0), 'bfloat16'), 'ra': ('dram', shape_of(0), 'bfloat16'), 'xb': ('dram', shape_of(1), 'bfloat16'), 'rb': ('dram', shape_of(1), 'bfloat16'), 'xc': ('dram', shape_of(2), 'bfloat16'), 'rc': ('dram', shape_of(2), 'bfloat16')}
+
+
+SCRATCH = {'xa': ('dram', shape_of(0), 'bfloat16'), 'ra': ('dram', shape_of(0), 'bfloat16'),
+           'xb': ('dram', shape_of(1), 'bfloat16'), 'rb': ('dram', shape_of(1), 'bfloat16'),
+           'xc': ('dram', shape_of(2), 'bfloat16'), 'rc': ('dram', shape_of(2), 'bfloat16')}
 SEMAPHORES = ['st', 'sent'] + ['s%d' % k for k in range(16)] + ['ld%d' % k for k in range(16)]
 
+
 def red_core(k, s):
-    if RAILS:
-        j, h = divmod(s, 2)
-        return (2 * j + 1) * 8 + (6 if h else 2) + k % 2
-    return 2 * s * 8 + 4 + (3 - k % NR)
+    j, h = divmod(s, 2)
+    return (2 * j + 1) * 8 + (6 if h else 2) + k % 2
+
 
 def fwd_core(rank_core, s):
-    if RAILS and s % 2:
+    if s % 2:
         return rank_core // 8 * 8 + 6 + s // 2 % 2
     return None
 
+
 def bits(first, n):
     return (1 << n) - 1 << first
+
 
 def rank_program(g, core, T, topo):
     sems = [T.sem.s0, T.sem.s1, T.sem.s2, T.sem.s3, T.sem.s4, T.sem.s5, T.sem.s6, T.sem.s7, T.sem.s8, T.sem.s9, T.sem.s10, T.sem.s11, T.sem.s12, T.sem.s13, T.sem.s14, T.sem.s15]
@@ -57,11 +61,9 @@ def rank_program(g, core, T, topo):
     sent = 0
     rank = T.rank_of(core)
     if rank is not None:
-
-        def load(k):
-            g.dma_start(xbuf[CLS[k]][IDX[k] * S:(IDX[k] + 1) * S], T.x[OFF[k]:OFF[k] + STAGES[k], :]).then_inc(lds[k], 16)
-        for k in range(min(PRE, K)):
-            load(k)
+        hw = [g.sync, g.scalar]
+        for k in range(K):
+            hw[k % 2].dma_start(xbuf[CLS[k]][IDX[k] * S:(IDX[k] + 1) * S], T.x[OFF[k]:OFF[k] + STAGES[k], :]).then_inc(lds[k], 16)
         for k in range(K):
             g.wait_ge(lds[k], 16)
             tr = []
@@ -72,13 +74,12 @@ def rank_program(g, core, T, topo):
                 tr.append(copy(piece(k, s), piece(k, s), fwd_core(core, s), bits(8 + n * e_pas, e_pas), sems[k]))
                 sent += e_pas
             g.remote_dma_fused(tr, local_sem=T.sem.sent)
-            if k + PRE < K:
-                load(k + PRE)
         for k in range(K):
-            g.wait_ge(sems[k], 8 * S)
-            g.dma_start(T.y[OFF[k]:OFF[k] + STAGES[k], :], rbuf[CLS[k]][IDX[k] * S:(IDX[k] + 1) * S]).then_inc(T.sem.st, 16)
-        g.wait_ge(T.sem.st, 16 * K)
+            q = hw[k % 2]
+            q.wait_ge(sems[k], 8 * S)
+            q.dma_start(T.y[OFF[k]:OFF[k] + STAGES[k], :], rbuf[CLS[k]][IDX[k] * S:(IDX[k] + 1) * S]).then_inc(T.sem.st, 16)
         g.wait_ge(T.sem.sent, sent)
+        g.wait_ge(T.sem.st, 16 * K)
         return
     home = [r for r in ranks if r // 8 == core // 8]
     mine = [s for s in passed if home and fwd_core(home[0], s) == core]

@@ -6,6 +6,7 @@ OFF = [sum(STAGES[:k]) for k in range(K)]
 SIZES = sorted(set(STAGES))
 CLS = [SIZES.index(r) for r in STAGES]
 IDX = [CLS[:k].count(CLS[k]) for k in range(K)]
+EVEN = [k % 4 == 3 for k in range(K)]
 
 
 def shape_of(c):
@@ -22,7 +23,10 @@ SEMAPHORES = ['st', 'sent'] + ['s%d' % k for k in range(16)] + ['ld%d' % k for k
 
 def red_core(k, s):
     j, h = divmod(s, 2)
-    return (2 * j + 1) * 8 + (6 if h else 2) + k % 2
+    turn = EVEN[:k].count(EVEN[k]) % 2
+    if EVEN[k]:
+        return (2 * j) * 8 + (4 if h else 0) + turn
+    return (2 * j + 1) * 8 + (6 if h else 2) + turn
 
 
 def fwd_core(rank_core, s):

@@ -1,23 +1,12 @@
 import concourse.bass as bass
-STAGES = [16] * 8
+R = 16
+K = 128 // R
 S = 16
-K = len(STAGES)
-OFF = [sum(STAGES[:k]) for k in range(K)]
-SIZES = sorted(set(STAGES))
-CLS = [SIZES.index(r) for r in STAGES]
-IDX = [CLS[:k].count(CLS[k]) for k in range(K)]
+PN = R * 8192 // (S * 128)
 EVEN = [k % 4 == 3 for k in range(K)]
+PRE = 4
 
-
-def shape_of(c):
-    if c >= len(SIZES):
-        return [1, 128, 1]
-    return [CLS.count(c) * S, 128, SIZES[c] * 8192 // (S * 128)]
-
-
-SCRATCH = {'xa': ('dram', shape_of(0), 'bfloat16'), 'ra': ('dram', shape_of(0), 'bfloat16'),
-           'xb': ('dram', shape_of(1), 'bfloat16'), 'rb': ('dram', shape_of(1), 'bfloat16'),
-           'xc': ('dram', shape_of(2), 'bfloat16'), 'rc': ('dram', shape_of(2), 'bfloat16')}
+SCRATCH = {'xa': ('dram', [K * S, 128, PN], 'bfloat16'), 'ra': ('dram', [K * S, 128, PN], 'bfloat16')}
 SEMAPHORES = ['st', 'sent'] + ['s%d' % k for k in range(16)] + ['ld%d' % k for k in range(16)]
 
 
@@ -42,15 +31,13 @@ def bits(first, n):
 def rank_program(g, core, T, topo):
     sems = [T.sem.s0, T.sem.s1, T.sem.s2, T.sem.s3, T.sem.s4, T.sem.s5, T.sem.s6, T.sem.s7, T.sem.s8, T.sem.s9, T.sem.s10, T.sem.s11, T.sem.s12, T.sem.s13, T.sem.s14, T.sem.s15]
     lds = [T.sem.ld0, T.sem.ld1, T.sem.ld2, T.sem.ld3, T.sem.ld4, T.sem.ld5, T.sem.ld6, T.sem.ld7, T.sem.ld8, T.sem.ld9, T.sem.ld10, T.sem.ld11, T.sem.ld12, T.sem.ld13, T.sem.ld14, T.sem.ld15]
-    xbuf = [T.xa, T.xb, T.xc]
-    rbuf = [T.ra, T.rb, T.rc]
     ranks = list(T.cores)
 
     def piece(k, s):
-        return xbuf[CLS[k]][IDX[k] * S + s]
+        return T.xa[k * S + s]
 
     def landed(k, i):
-        return xbuf[CLS[k]][IDX[k] * 8 + i]
+        return T.xa[k * 8 + i]
 
     def did(c):
         rid, pid, se = topo.addr(c)
@@ -67,7 +54,9 @@ def rank_program(g, core, T, topo):
     if rank is not None:
         hw = [g.sync, g.scalar]
         for k in range(K):
-            hw[k % 2].dma_start(xbuf[CLS[k]][IDX[k] * S:(IDX[k] + 1) * S], T.x[OFF[k]:OFF[k] + STAGES[k], :]).then_inc(lds[k], 16)
+            if k >= PRE:
+                hw[k % 2].wait_ge(lds[k - PRE], 16)
+            hw[k % 2].dma_start(T.xa[k * S:(k + 1) * S], T.x[k * R:(k + 1) * R, :]).then_inc(lds[k], 16)
         for k in range(K):
             g.wait_ge(lds[k], 16)
             tr = []
@@ -81,7 +70,7 @@ def rank_program(g, core, T, topo):
         for k in range(K):
             q = hw[k % 2]
             q.wait_ge(sems[k], 8 * S)
-            q.dma_start(T.y[OFF[k]:OFF[k] + STAGES[k], :], rbuf[CLS[k]][IDX[k] * S:(IDX[k] + 1) * S]).then_inc(T.sem.st, 16)
+            q.dma_start(T.y[k * R:(k + 1) * R, :], T.ra[k * S:(k + 1) * S]).then_inc(T.sem.st, 16)
         g.wait_ge(T.sem.sent, sent)
         g.wait_ge(T.sem.st, 16 * K)
         return
@@ -103,7 +92,7 @@ def rank_program(g, core, T, topo):
             if red_core(k, s) != core:
                 continue
             g.wait_ge(sems[k], 8 * (e_dir if s in direct else 8 // n_fwd))
-            g.remote_dma_fused([bass.RemoteDMATransfer(dst_ids=[did(r) for r in ranks], dma_engine_mask=255, remote_sem=sems[k], srcs=[landed(k, i) for i in range(8)], dsts=[rbuf[CLS[k]][IDX[k] * S + s] for r in ranks], alu_op=1)], local_sem=T.sem.sent)
+            g.remote_dma_fused([bass.RemoteDMATransfer(dst_ids=[did(r) for r in ranks], dma_engine_mask=255, remote_sem=sems[k], srcs=[landed(k, i) for i in range(8)], dsts=[T.ra[k * S + s] for r in ranks], alu_op=1)], local_sem=T.sem.sent)
             sent += 8
     if sent:
         g.wait_ge(T.sem.sent, sent)

@@ -1,27 +1,26 @@
 import concourse.bass as bass
-R = 16
-K = 128 // R
-S = 16
-PN = R * 8192 // (S * 128)
-EVEN = [k % 4 == 3 for k in range(K)]
+NB = 16
+RB = 8
+PN = RB * 8192 // (8 * 128)
+ISF = [p in (0, 1, 2, 4, 6, 8, 10, 12) for p in range(NB)]
+EVEN = [p in (4, 9, 12, 15) for p in range(NB)]
+CALLS = [(0, 2), (2, 4), (4, 6), (6, 8), (8, 10), (10, 12), (12, 14), (14, 15), (15, 16)]
+LOADS = [(0, 2), (2, 4), (4, 6), (6, 8), (8, 10), (10, 12), (12, 14), (14, 16)]
 PRE = 4
 
-SCRATCH = {'xa': ('dram', [K * S, 128, PN], 'bfloat16'), 'ra': ('dram', [K * S, 128, PN], 'bfloat16')}
+SCRATCH = {'xa': ('dram', [NB * 8, 128, PN], 'bfloat16'), 'ra': ('dram', [NB * 8, 128, PN], 'bfloat16')}
 SEMAPHORES = ['st', 'sent'] + ['s%d' % k for k in range(16)] + ['ld%d' % k for k in range(16)]
 
 
-def red_core(k, s):
-    j, h = divmod(s, 2)
-    turn = EVEN[:k].count(EVEN[k]) % 2
-    if EVEN[k]:
-        return (2 * j) * 8 + (4 if h else 0) + turn
-    return (2 * j + 1) * 8 + (6 if h else 2) + turn
+def red_core(p, q):
+    turn = len([t for t in range(p) if EVEN[t] == EVEN[p] and ISF[t] == ISF[p]]) % 2
+    if EVEN[p]:
+        return (2 * q) * 8 + (4 if ISF[p] else 0) + turn
+    return (2 * q + 1) * 8 + (6 if ISF[p] else 2) + turn
 
 
-def fwd_core(rank_core, s):
-    if s % 2:
-        return rank_core // 8 * 8 + 6 + s // 2 % 2
-    return None
+def fwd_core(rank_core, q):
+    return rank_core // 8 * 8 + 6 + q % 2
 
 
 def bits(first, n):
@@ -33,66 +32,65 @@ def rank_program(g, core, T, topo):
     lds = [T.sem.ld0, T.sem.ld1, T.sem.ld2, T.sem.ld3, T.sem.ld4, T.sem.ld5, T.sem.ld6, T.sem.ld7, T.sem.ld8, T.sem.ld9, T.sem.ld10, T.sem.ld11, T.sem.ld12, T.sem.ld13, T.sem.ld14, T.sem.ld15]
     ranks = list(T.cores)
 
-    def piece(k, s):
-        return T.xa[k * S + s]
-
-    def landed(k, i):
-        return T.xa[k * 8 + i]
-
     def did(c):
         rid, pid, se = topo.addr(c)
         return bass.DstId(rid=rid, pnc=pid)
 
     def copy(src, dst, dst_core, mask, sem):
         return bass.RemoteDMATransfer(dst_ids=[did(dst_core)], dma_engine_mask=mask, remote_sem=sem, src=src, dst=dst)
-    direct = [s for s in range(S) if fwd_core(ranks[0], s) is None]
-    passed = [s for s in range(S) if fwd_core(ranks[0], s) is not None]
-    e_dir = 8 // len(direct)
-    e_pas = 8 // len(passed) if passed else 0
     sent = 0
     rank = T.rank_of(core)
     if rank is not None:
         hw = [g.sync, g.scalar]
-        for k in range(K):
-            if k >= PRE:
-                hw[k % 2].wait_ge(lds[k - PRE], 16)
-            hw[k % 2].dma_start(T.xa[k * S:(k + 1) * S], T.x[k * R:(k + 1) * R, :]).then_inc(lds[k], 16)
-        for k in range(K):
-            g.wait_ge(lds[k], 16)
+        for n, (a, b) in enumerate(LOADS):
+            if n >= PRE:
+                hw[n % 2].wait_ge(lds[n - PRE], 16)
+            hw[n % 2].dma_start(T.xa[a * 8:b * 8], T.x[a * RB:b * RB, :]).then_inc(lds[n], 16)
+        waited = -1
+        for a, b in CALLS:
+            n = [i for i, (la, lb) in enumerate(LOADS) if la <= a < lb][0]
+            if n > waited:
+                g.wait_ge(lds[n], 16)
+                waited = n
             tr = []
-            for n, s in enumerate(direct):
-                tr.append(copy(piece(k, s), landed(k, rank), red_core(k, s), bits(n * e_dir, e_dir), sems[k]))
-                sent += e_dir
-            for n, s in enumerate(passed):
-                tr.append(copy(piece(k, s), piece(k, s), fwd_core(core, s), bits(8 + n * e_pas, e_pas), sems[k]))
-                sent += e_pas
+            high = 8
+            for p in range(a, b):
+                for q in range(8):
+                    if ISF[p]:
+                        tr.append(copy(T.xa[p * 8 + q], T.xa[p * 8 + q], fwd_core(core, q), bits(high + q, 1), sems[p]))
+                    else:
+                        tr.append(copy(T.xa[p * 8 + q], T.xa[p * 8 + rank], red_core(p, q), bits(q, 1), sems[p]))
+                    sent += 1
+                if ISF[p]:
+                    high = 0
             g.remote_dma_fused(tr, local_sem=T.sem.sent)
-        for k in range(K):
-            q = hw[k % 2]
-            q.wait_ge(sems[k], 8 * S)
-            q.dma_start(T.y[k * R:(k + 1) * R, :], T.ra[k * S:(k + 1) * S]).then_inc(T.sem.st, 16)
+        for n, (a, b) in enumerate(CALLS):
+            q = hw[n % 2]
+            for p in range(a, b):
+                q.wait_ge(sems[p], 64)
+            q.dma_start(T.y[a * RB:b * RB, :], T.ra[a * 8:b * 8]).then_inc(T.sem.st, 16)
         g.wait_ge(T.sem.sent, sent)
-        g.wait_ge(T.sem.st, 16 * K)
+        g.wait_ge(T.sem.st, 16 * len(CALLS))
         return
     home = [r for r in ranks if r // 8 == core // 8]
-    mine = [s for s in passed if home and fwd_core(home[0], s) == core]
+    mine = [q for q in range(8) if home and fwd_core(home[0], q) == core]
     if mine:
-        e_fwd = 8 // len(mine)
         i = T.rank_of(home[0])
-        for k in range(K):
-            g.wait_ge(sems[k], e_pas * len(mine))
-            tr = [copy(piece(k, s), landed(k, i), red_core(k, s), bits(n * e_fwd, e_fwd), sems[k]) for n, s in enumerate(mine)]
-            sent += e_fwd * len(mine)
+        for p in range(NB):
+            if not ISF[p]:
+                continue
+            g.wait_ge(sems[p], len(mine))
+            tr = [copy(T.xa[p * 8 + q], T.xa[p * 8 + i], red_core(p, q), bits(n * 2, 2), sems[p]) for n, q in enumerate(mine)]
+            sent += 2 * len(mine)
             g.remote_dma_fused(tr, local_sem=T.sem.sent)
         g.wait_ge(T.sem.sent, sent)
         return
-    n_fwd = len([s for s in passed if fwd_core(ranks[0], s) == fwd_core(ranks[0], passed[0])]) if passed else 1
-    for k in range(K):
-        for s in range(S):
-            if red_core(k, s) != core:
+    for p in range(NB):
+        for q in range(8):
+            if red_core(p, q) != core:
                 continue
-            g.wait_ge(sems[k], 8 * (e_dir if s in direct else 8 // n_fwd))
-            g.remote_dma_fused([bass.RemoteDMATransfer(dst_ids=[did(r) for r in ranks], dma_engine_mask=255, remote_sem=sems[k], srcs=[landed(k, i) for i in range(8)], dsts=[T.ra[k * S + s] for r in ranks], alu_op=1)], local_sem=T.sem.sent)
+            g.wait_ge(sems[p], 8 * (2 if ISF[p] else 1))
+            g.remote_dma_fused([bass.RemoteDMATransfer(dst_ids=[did(r) for r in ranks], dma_engine_mask=255, remote_sem=sems[p], srcs=[T.xa[p * 8 + i] for i in range(8)], dsts=[T.ra[p * 8 + q] for r in ranks], alu_op=1)], local_sem=T.sem.sent)
             sent += 8
     if sent:
         g.wait_ge(T.sem.sent, sent)

import concourse.bass as bass
NB = 16
RB = 8
PN = RB * 8192 // (8 * 128)
ISF = [p in (0, 1, 2, 4, 6, 8, 10, 12) for p in range(NB)]
EVEN = [p in (4, 9, 12, 15) for p in range(NB)]
CALLS = [(0, 2), (2, 4), (4, 6), (6, 8), (8, 10), (10, 12), (12, 14), (14, 15), (15, 16)]
LOADS = [(0, 2), (2, 4), (4, 6), (6, 8), (8, 10), (10, 12), (12, 14), (14, 16)]
PRE = 4

SCRATCH = {'xa': ('dram', [NB * 8, 128, PN], 'bfloat16'), 'ra': ('dram', [NB * 8, 128, PN], 'bfloat16')}
SEMAPHORES = ['st', 'sent'] + ['s%d' % k for k in range(16)] + ['ld%d' % k for k in range(16)]


def red_core(p, q):
    turn = len([t for t in range(p) if EVEN[t] == EVEN[p] and ISF[t] == ISF[p]]) % 2
    if EVEN[p]:
        return (2 * q) * 8 + (4 if ISF[p] else 0) + turn
    return (2 * q + 1) * 8 + (6 if ISF[p] else 2) + turn


def fwd_core(rank_core, q):
    return rank_core // 8 * 8 + 6 + q % 2


def bits(first, n):
    return (1 << n) - 1 << first


def rank_program(g, core, T, topo):
    sems = [T.sem.s0, T.sem.s1, T.sem.s2, T.sem.s3, T.sem.s4, T.sem.s5, T.sem.s6, T.sem.s7, T.sem.s8, T.sem.s9, T.sem.s10, T.sem.s11, T.sem.s12, T.sem.s13, T.sem.s14, T.sem.s15]
    lds = [T.sem.ld0, T.sem.ld1, T.sem.ld2, T.sem.ld3, T.sem.ld4, T.sem.ld5, T.sem.ld6, T.sem.ld7, T.sem.ld8, T.sem.ld9, T.sem.ld10, T.sem.ld11, T.sem.ld12, T.sem.ld13, T.sem.ld14, T.sem.ld15]
    ranks = list(T.cores)

    def did(c):
        rid, pid, se = topo.addr(c)
        return bass.DstId(rid=rid, pnc=pid)

    def copy(src, dst, dst_core, mask, sem):
        return bass.RemoteDMATransfer(dst_ids=[did(dst_core)], dma_engine_mask=mask, remote_sem=sem, src=src, dst=dst)
    sent = 0
    rank = T.rank_of(core)
    if rank is not None:
        hw = [g.sync, g.scalar]
        for n, (a, b) in enumerate(LOADS):
            if n >= PRE:
                hw[n % 2].wait_ge(lds[n - PRE], 16)
            hw[n % 2].dma_start(T.xa[a * 8:b * 8], T.x[a * RB:b * RB, :]).then_inc(lds[n], 16)
        waited = -1
        for a, b in CALLS:
            n = [i for i, (la, lb) in enumerate(LOADS) if la <= a < lb][0]
            if n > waited:
                g.wait_ge(lds[n], 16)
                waited = n
            tr = []
            high = 8
            for p in range(a, b):
                for q in range(8):
                    if ISF[p]:
                        tr.append(copy(T.xa[p * 8 + q], T.xa[p * 8 + q], fwd_core(core, q), bits(high + q, 1), sems[p]))
                    else:
                        tr.append(copy(T.xa[p * 8 + q], T.xa[p * 8 + rank], red_core(p, q), bits(q, 1), sems[p]))
                    sent += 1
                if ISF[p]:
                    high = 0
            g.remote_dma_fused(tr, local_sem=T.sem.sent)
        for n, (a, b) in enumerate(CALLS):
            q = hw[n % 2]
            for p in range(a, b):
                q.wait_ge(sems[p], 64)
            q.dma_start(T.y[a * RB:b * RB, :], T.ra[a * 8:b * 8]).then_inc(T.sem.st, 16)
        g.wait_ge(T.sem.sent, sent)
        g.wait_ge(T.sem.st, 16 * len(CALLS))
        return
    home = [r for r in ranks if r // 8 == core // 8]
    mine = [q for q in range(8) if home and fwd_core(home[0], q) == core]
    if mine:
        i = T.rank_of(home[0])
        for p in range(NB):
            if not ISF[p]:
                continue
            g.wait_ge(sems[p], len(mine))
            tr = [copy(T.xa[p * 8 + q], T.xa[p * 8 + i], red_core(p, q), bits(n * 2, 2), sems[p]) for n, q in enumerate(mine)]
            sent += 2 * len(mine)
            g.remote_dma_fused(tr, local_sem=T.sem.sent)
        g.wait_ge(T.sem.sent, sent)
        return
    for p in range(NB):
        for q in range(8):
            if red_core(p, q) != core:
                continue
            g.wait_ge(sems[p], 8 * (2 if ISF[p] else 1))
            g.remote_dma_fused([bass.RemoteDMATransfer(dst_ids=[did(r) for r in ranks], dma_engine_mask=255, remote_sem=sems[p], srcs=[T.xa[p * 8 + i] for i in range(8)], dsts=[T.ra[p * 8 + q] for r in ranks], alu_op=1)], local_sem=T.sem.sent)
            sent += 8
    if sent:
        g.wait_ge(T.sem.sent, sent)
